import numpy as np
import ml_dtypes


def mxq(x, axis, fmt="e4m3"):
    dtype, down = {"e4m3": (ml_dtypes.float8_e4m3fn, 7), "e5m2": (ml_dtypes.float8_e5m2, 14)}[fmt]
    v = np.moveaxis(np.asarray(x, np.float32).astype(ml_dtypes.bfloat16).astype(np.float64), axis, -1)
    blocks = v.reshape(v.shape[:-1] + (-1, 32))
    amax = np.abs(blocks).max(-1, keepdims=True)
    byte = np.maximum(np.where(amax > 0, np.frexp(amax)[1] - 1 + 127, 0) - down, 1)
    scale = np.exp2(byte - 127.0)
    codes = (blocks / scale).astype(np.float32).astype(dtype).astype(np.float64)
    return np.moveaxis((codes * scale).reshape(v.shape), -1, axis)


WIDE = False


def mx_kscale(k):
    if not WIDE:
        return np.ones(k)
    levels = np.array([24, -24, 12, -12, 0])
    if k % 512:
        return np.exp2(np.random.permutation(np.resize(levels, k // 32))).repeat(32)
    a = np.empty((k // 512, 16))
    for p in range(k // 512):
        a[p, :8] = np.random.permutation(np.resize(levels, 8))
        for g in range(8):
            far = levels[np.abs(levels - a[p, g]) >= 10]
            a[p, g + 8] = far[np.random.randint(len(far))]
    return np.exp2(a.ravel()).repeat(32)


def f64(x):
    return np.asarray(x).astype(np.float64)


E2M1 = np.array([0.0, 0.5, 1.0, 1.5, 2.0, 3.0, 4.0, 6.0, -0.0, -0.5, -1.0, -1.5, -2.0, -3.0, -4.0, -6.0])


def pack_weight(w, fmt):
    k, n = w.shape
    w = f64(np.asarray(w, np.float32).astype(ml_dtypes.bfloat16)).reshape(k // 32, 32, n)
    amax = np.abs(w).max(1)
    if fmt == "e4m3":
        byte = np.frexp(amax)[1] - 1 + 127 - 7
    else:
        mant, ex = np.frexp(amax / 6.0)
        byte = np.where(mant > 0.5, ex, ex - 1) + 127
    byte = np.clip(np.where(amax > 0, byte, 1), 1, 254)
    scaled = (w * np.exp2(127.0 - byte)[:, None, :]).reshape(k, n).astype(np.float32)
    by_word = np.ascontiguousarray(scaled.reshape(k // 512, 128, 4, n).transpose(0, 1, 3, 2))
    if fmt == "e4m3":
        words = by_word.astype(ml_dtypes.float8_e4m3fn).view(np.uint8)
    else:
        c = by_word.astype(ml_dtypes.float4_e2m1fn).view(np.uint8) & 0xF
        words = (c[..., 0::2] | (c[..., 1::2] << 4)).reshape(k // 512, 128, 2 * n)
    return np.ascontiguousarray(words), np.ascontiguousarray(byte.astype(np.uint8).reshape(k // 512, 16, n))


def unpack_weight(words, scales, fmt):
    g, _, n = scales.shape
    words = np.ascontiguousarray(words).reshape(g, 128, n, -1)
    if fmt == "e4m3":
        vals = words.view(ml_dtypes.float8_e4m3fn).astype(np.float64)
    else:
        nib = np.empty((g, 128, n, 4), np.uint8)
        nib[..., 0::2] = words & 0xF
        nib[..., 1::2] = words >> 4
        vals = E2M1[nib]
    vals = vals * np.repeat(np.exp2(scales.astype(np.float64) - 127.0), 8, axis=1)[..., None]
    return vals.transpose(0, 1, 3, 2).reshape(g * 512, n)


def sigm(f):
    return 1.0 / (1.0 + np.exp(-np.maximum(f, -700.0)))


K, N, T = 512, 512, 1536


def setup_inputs():
    n = np.random.standard_normal
    s = mx_kscale(K)[:, None]
    p_wg = pack_weight(n((K, N)) / np.sqrt(K) / s, "e4m3")
    return {
        "x": (n((K, T)) * s).astype(np.float32),
        "wg_words": p_wg[0],
        "wg_scales": p_wg[1],
        "wh": (n((K, N)) / np.sqrt(K) / s).astype(np.float32),
        "bg": (0.3 * n(N) - 1.0).astype(np.float32),
        "res": (n((N, T))).astype(np.float32),
    }


def reference(x, wg_words, wg_scales, wh, bg, res):
    x_ = mxq(f64(x), 0, "e4m3")
    wg_ = unpack_weight(wg_words, wg_scales, "e4m3")
    wh_ = mxq(f64(wh), 0, "e4m3")
    ga = wg_.T @ x_
    gate = sigm(ga + f64(bg)[:, None])
    ha = wh_.T @ x_
    return f64(res) + gate * (np.tanh(ha) - f64(res))

@@ -1,0 +1,244 @@
+from contextlib import ExitStack
+
+import concourse.mybir as mybir
+from concourse.masks import make_identity
+
+K, N, T = 512, 512, 1536
+FLOPS = 2 * 2 * K * N * T
+
+F32 = mybir.dt.float32
+BF16 = mybir.dt.bfloat16
+I32 = mybir.dt.int32
+U32 = mybir.dt.uint32
+U8 = mybir.dt.uint8
+FP8X4 = mybir.dt.float8_e4m3fn_x4
+ACT = mybir.ActivationFunctionType
+ALU = mybir.AluOpType
+
+P = 128
+PACK = 4
+CHUNK = 512
+HALF = 256
+N_TILES = N // P
+CHUNKS = T // CHUNK
+UNITS = CHUNKS * N_TILES
+BLEND_LAG = 2
+TANH_BANKS = 4
+VECTOR_GATED = (UNITS - 1,)
+
+
+def tile_mix_hway_tanh_none_kernel(tc, x, wg_words, wg_scales, wh, bg, res, out):
+    nc = tc.nc
+    with ExitStack() as ctx:
+        sb = ctx.enter_context(tc.tile_pool(name="sb", bufs=1))
+        ps = ctx.enter_context(tc.psum_pool(name="ps", bufs=1))
+        ctx.enter_context(tc.manual_schedule())
+
+        ident = sb.tile([P, P], F32, name="ident")
+        make_identity(nc, ident[:])
+        wg_plane = sb.tile([P, N], U8, name="wg_plane", align_bytes=64)
+        nc.vector.memset(wg_plane[:].bitcast(U32), 0)
+        bias_rows = sb.tile([P, P], F32, name="bias_rows")
+        nc.vector.memset(bias_rows[:], 0.0)
+
+        warm = sb.tile([P, 1], F32, name="warm")
+        nc.scalar.activation(out=warm[:], in_=ident[:, 0:1], func=ACT.Sigmoid)
+
+        x_raw = {}
+        res_sb = {}
+
+        def load_x(c):
+            x_raw[c] = sb.tile([P, PACK, CHUNK], F32, name="x_raw%d" % c)
+            nc.sync.dma_start(
+                out=x_raw[c][:],
+                in_=x.rearrange("(p j) t -> p j t", j=PACK)[:, :, c * CHUNK:(c + 1) * CHUNK],
+            )
+
+        def load_res(u):
+            c, j = divmod(u, N_TILES)
+            res_sb[u] = sb.tile([P, CHUNK], F32, name="res%d" % u)
+            nc.sync.dma_start(out=res_sb[u][:], in_=res[j * P:(j + 1) * P, c * CHUNK:(c + 1) * CHUNK])
+
+        wh_raw = {}
+
+        def load_wh(h):
+            wh_raw[h] = sb.tile([P, PACK, HALF], F32, name="wh_raw%d" % h)
+            nc.sync.dma_start(
+                out=wh_raw[h][:], in_=wh.rearrange("(p j) n -> p j n", j=PACK)[:, :, h * HALF:(h + 1) * HALF]
+            )
+
+        load_x(0)
+        load_wh(0)
+        nc.sync.dma_start(out=bias_rows[0:N_TILES, :], in_=bg.rearrange("(j p) -> j p", p=P))
+        for q in range(4):
+            nc.sync.dma_start(
+                out=wg_plane[32 * q:32 * q + 4, :].bitcast(I32),
+                in_=wg_scales[0, 4 * q:4 * q + 4, :].bitcast(I32),
+            )
+        wg_codes = sb.tile([P, N * PACK], U8, name="wg_codes", align_bytes=64)
+        nc.sync.dma_start(
+            out=wg_codes[:].bitcast(I32),
+            in_=wg_words[0].rearrange("p n t -> p (n t)").bitcast(I32),
+        )
+        load_wh(1)
+        load_res(0)
+        load_res(1)
+        load_x(1)
+        for u in range(2, 5):
+            load_res(u)
+        load_x(2)
+        for u in range(5, UNITS):
+            load_res(u)
+
+        grouped = {}
+
+        def interleave(key, raw_half, h, on_scalar):
+            grouped[key, h] = sb.tile([P, HALF * PACK], BF16, name="grouped_%s%d" % (key, h), align_bytes=64)
+            dst = grouped[key, h][:].rearrange("p (c i j) -> p c j i", i=4, j=PACK)
+            src = raw_half.rearrange("p j (c i) -> p c j i", i=4)
+            if on_scalar:
+                nc.scalar.copy(out=dst, in_=src)
+            else:
+                nc.vector.tensor_copy(out=dst, in_=src)
+
+        codes = {}
+        scales = {}
+
+        def quantize(key, h):
+            if h == 0:
+                codes[key] = sb.tile([P, 2 * HALF], U32, name="codes_%s" % key, align_bytes=64)
+                scales[key] = sb.tile([P, 2 * HALF], U8, name="scales_%s" % key, align_bytes=64)
+            cols = slice(h * HALF, (h + 1) * HALF)
+            nc.vector.quantize_mx(
+                out=codes[key][:, cols].bitcast(FP8X4), scales=scales[key][:, cols], in_=grouped[key, h][:]
+            )
+
+        def interleave_x(c, h, on_scalar):
+            interleave("x%d" % c, x_raw[c][:, :, h * HALF:(h + 1) * HALF], h, on_scalar)
+
+        interleave_x(0, 0, False)
+        interleave_x(0, 1, True)
+        quantize("x0", 0)
+        interleave("wh", wh_raw[0][:], 0, False)
+        quantize("x0", 1)
+        quantize("wh", 0)
+        bias_ps = ps.tile([P, CHUNK], F32, name="bias_ps", tag="tanh%d" % (TANH_BANKS - 1))
+        nc.tensor.transpose(bias_ps[:, 0:P], bias_rows[:], ident[:])
+        neg_bias = sb.tile([P, N_TILES], F32, name="neg_bias")
+        nc.vector.tensor_scalar(
+            out=neg_bias[:], in0=bias_ps[:, 0:N_TILES], scalar1=-1.0, scalar2=None, op0=ALU.mult
+        )
+
+        out_sb = [sb.tile([P, T], F32, name="out%d" % j) for j in range(N_TILES)]
+        tanh_t = {}
+        carry = {}
+        tanh_ps = {}
+        diff = {}
+        kept = {}
+
+        def products(u):
+            c, j = divmod(u, N_TILES)
+            key = "x%d" % c
+            n_cols = slice(j * P, (j + 1) * P)
+            ga = ps.tile([P, CHUNK], F32, name="ga%d" % u, tag="ga%d" % (u % 2))
+            ha = ps.tile([P, CHUNK], F32, name="ha%d" % u, tag="ha%d" % (u % 2))
+            for b in range(CHUNK // P):
+                t_cols = slice(b * P, (b + 1) * P)
+                nc.tensor.matmul_mx(
+                    out=ha[:, t_cols],
+                    lhsT=codes[key][:, t_cols].bitcast(FP8X4),
+                    lhsT_scale=scales[key][:, t_cols],
+                    rhs=codes["wh"][:, n_cols].bitcast(FP8X4),
+                    rhs_scale=scales["wh"][:, n_cols],
+                    start=True,
+                    stop=True,
+                )
+            nc.tensor.matmul_mx(
+                out=ga[:],
+                lhsT=wg_codes[:, j * P * PACK:(j + 1) * P * PACK].bitcast(FP8X4),
+                lhsT_scale=wg_plane[:, n_cols],
+                rhs=codes[key][:].bitcast(FP8X4),
+                rhs_scale=scales[key][:],
+                start=True,
+                stop=True,
+            )
+            tanh_t[u] = sb.tile([P, CHUNK], F32, name="tanh_t%d" % u)
+            carry[u] = sb.tile([P, CHUNK], F32, name="carry%d" % u)
+            nc.scalar.activation(out=tanh_t[u][:], in_=ha[:], func=ACT.Tanh)
+            nc.scalar.activation(out=carry[u][:], in_=ga[:], func=ACT.Sigmoid, bias=neg_bias[:, j:j + 1], scale=-1.0)
+
+        def turn(u):
+            tanh_ps[u] = ps.tile([P, CHUNK], F32, name="tanh_ps%d" % u, tag="tanh%d" % (u % TANH_BANKS))
+            for b in range(CHUNK // P):
+                cols = slice(b * P, (b + 1) * P)
+                nc.tensor.transpose(tanh_ps[u][:, cols], tanh_t[u][:, cols], ident[:])
+
+        def subtract(u):
+            diff[u] = sb.tile([P, CHUNK], F32, name="diff%d" % u)
+            nc.vector.tensor_tensor(out=diff[u][:], in0=tanh_ps[u][:], in1=res_sb[u][:], op=ALU.subtract)
+
+        def gate(u):
+            kept[u] = sb.tile([P, CHUNK], F32, name="kept%d" % u)
+            engine = nc.vector if u in VECTOR_GATED else nc.gpsimd
+            engine.tensor_tensor(out=kept[u][:], in0=diff[u][:], in1=carry[u][:], op=ALU.mult)
+
+        def blend(u):
+            c, j = divmod(u, N_TILES)
+            nc.vector.tensor_tensor(
+                out=out_sb[j][:, c * CHUNK:(c + 1) * CHUNK], in0=tanh_ps[u][:], in1=kept[u][:], op=ALU.subtract
+            )
+
+        products(0)
+        products(1)
+        interleave("wh", wh_raw[1][:], 1, False)
+        quantize("wh", 1)
+        turn(0)
+        subtract(0)
+        gate(0)
+        products(2)
+        turn(1)
+        subtract(1)
+        gate(1)
+        blend(0)
+        products(3)
+        interleave_x(1, 1, True)
+        blend(1)
+        interleave_x(1, 0, False)
+        quantize("x1", 0)
+        turn(2)
+        turn(3)
+        quantize("x1", 1)
+        products(4)
+        subtract(2)
+        gate(2)
+        subtract(3)
+        gate(3)
+        products(5)
+        blend(2)
+        for u in range(4, UNITS):
+            turn(u)
+            subtract(u)
+            if u not in VECTOR_GATED:
+                gate(u)
+            if u == 4:
+                blend(3)
+                interleave_x(2, 0, False)
+                interleave_x(2, 1, True)
+            if u == 5:
+                quantize("x2", 0)
+            if u >= 4 + BLEND_LAG:
+                blend(u - BLEND_LAG)
+            if u == 6:
+                quantize("x2", 1)
+            if u + 2 < UNITS:
+                products(u + 2)
+            if u in VECTOR_GATED:
+                gate(u)
+        for u in range(UNITS - BLEND_LAG, UNITS):
+            blend(u)
+
+        first = (CHUNKS - 1) * CHUNK
+        for j in range(N_TILES):
+            nc.sync.dma_start(out=out[j * P:(j + 1) * P, 0:first], in_=out_sb[j][:, 0:first])
+        for j in range(N_TILES):
+            nc.sync.dma_start(out=out[j * P:(j + 1) * P, first:T], in_=out_sb[j][:, first:T])

@@ -24,7 +24,8 @@ CHUNKS = T // CHUNK
 UNITS = CHUNKS * N_TILES
 BLEND_LAG = 2
 TANH_BANKS = 4
-VECTOR_GATED = (UNITS - 1,)
+VECTOR_GATED = ()
+DIRECT = ()
 
 
 def tile_mix_hway_tanh_none_kernel(tc, x, wg_words, wg_scales, wh, bg, res, out):
@@ -61,73 +62,77 @@ def tile_mix_hway_tanh_none_kernel(tc, x, wg_words, wg_scales, wh, bg, res, out)
 
         wh_raw = {}
 
-        def load_wh(h):
-            wh_raw[h] = sb.tile([P, PACK, HALF], F32, name="wh_raw%d" % h)
+        def load_wh(lo, hi):
+            wh_raw[lo] = sb.tile([P, PACK, hi - lo], F32, name="wh_raw%d" % lo)
+            nc.sync.dma_start(out=wh_raw[lo][:], in_=wh.rearrange("(p j) n -> p j n", j=PACK)[:, :, lo:hi])
+
+        wg_codes = sb.tile([P, N * PACK], U8, name="wg_codes", align_bytes=64)
+
+        def load_wg():
+            nc.sync.dma_start(out=bias_rows[0:N_TILES, :], in_=bg.rearrange("(j p) -> j p", p=P))
+            for q in range(4):
+                nc.sync.dma_start(
+                    out=wg_plane[32 * q:32 * q + 4, :].bitcast(I32),
+                    in_=wg_scales[0, 4 * q:4 * q + 4, :].bitcast(I32),
+                )
             nc.sync.dma_start(
-                out=wh_raw[h][:], in_=wh.rearrange("(p j) n -> p j n", j=PACK)[:, :, h * HALF:(h + 1) * HALF]
+                out=wg_codes[:].bitcast(I32),
+                in_=wg_words[0].rearrange("p n t -> p (n t)").bitcast(I32),
             )
 
         load_x(0)
-        load_wh(0)
-        nc.sync.dma_start(out=bias_rows[0:N_TILES, :], in_=bg.rearrange("(j p) -> j p", p=P))
-        for q in range(4):
-            nc.sync.dma_start(
-                out=wg_plane[32 * q:32 * q + 4, :].bitcast(I32),
-                in_=wg_scales[0, 4 * q:4 * q + 4, :].bitcast(I32),
-            )
-        wg_codes = sb.tile([P, N * PACK], U8, name="wg_codes", align_bytes=64)
-        nc.sync.dma_start(
-            out=wg_codes[:].bitcast(I32),
-            in_=wg_words[0].rearrange("p n t -> p (n t)").bitcast(I32),
-        )
-        load_wh(1)
+        load_wg()
+        load_wh(0, 512)
+        load_x(1)
         load_res(0)
         load_res(1)
-        load_x(1)
-        for u in range(2, 5):
-            load_res(u)
         load_x(2)
-        for u in range(5, UNITS):
-            load_res(u)
+        load_res(2)
+        load_res(3)
+        load_res(4)
+        load_res(5)
+        load_res(6)
+        load_res(7)
+        load_res(8)
+        load_res(9)
+        load_res(10)
+        load_res(11)
 
         grouped = {}
+        codes = {}
+        scales = {}
+        for key in ("x0", "x1", "x2", "wh"):
+            codes[key] = sb.tile([P, CHUNK], U32, name="codes_%s" % key, align_bytes=64)
+            scales[key] = sb.tile([P, CHUNK], U8, name="scales_%s" % key, align_bytes=64)
 
-        def interleave(key, raw_half, h, on_scalar):
-            grouped[key, h] = sb.tile([P, HALF * PACK], BF16, name="grouped_%s%d" % (key, h), align_bytes=64)
-            dst = grouped[key, h][:].rearrange("p (c i j) -> p c j i", i=4, j=PACK)
-            src = raw_half.rearrange("p j (c i) -> p c j i", i=4)
+        def interleave(key, raw, lo, hi, on_scalar, base=0):
+            grouped[key, lo] = sb.tile([P, (hi - lo) * PACK], BF16, name="grouped_%s_%d" % (key, lo), align_bytes=64)
+            dst = grouped[key, lo][:].rearrange("p (c i j) -> p c j i", i=4, j=PACK)
+            src = raw[:, :, lo - base:hi - base].rearrange("p j (c i) -> p c j i", i=4)
             if on_scalar:
                 nc.scalar.copy(out=dst, in_=src)
             else:
                 nc.vector.tensor_copy(out=dst, in_=src)
 
-        codes = {}
-        scales = {}
-
-        def quantize(key, h):
-            if h == 0:
-                codes[key] = sb.tile([P, 2 * HALF], U32, name="codes_%s" % key, align_bytes=64)
-                scales[key] = sb.tile([P, 2 * HALF], U8, name="scales_%s" % key, align_bytes=64)
-            cols = slice(h * HALF, (h + 1) * HALF)
+        def quantize(key, lo, hi):
             nc.vector.quantize_mx(
-                out=codes[key][:, cols].bitcast(FP8X4), scales=scales[key][:, cols], in_=grouped[key, h][:]
+                out=codes[key][:, lo:hi].bitcast(FP8X4), scales=scales[key][:, lo:hi], in_=grouped[key, lo][:]
             )
 
-        def interleave_x(c, h, on_scalar):
-            interleave("x%d" % c, x_raw[c][:, :, h * HALF:(h + 1) * HALF], h, on_scalar)
+        def il(c, lo, hi, on_scalar):
+            interleave("x%d" % c, x_raw[c], lo, hi, on_scalar)
 
-        interleave_x(0, 0, False)
-        interleave_x(0, 1, True)
-        quantize("x0", 0)
-        interleave("wh", wh_raw[0][:], 0, False)
-        quantize("x0", 1)
-        quantize("wh", 0)
-        bias_ps = ps.tile([P, CHUNK], F32, name="bias_ps", tag="tanh%d" % (TANH_BANKS - 1))
-        nc.tensor.transpose(bias_ps[:, 0:P], bias_rows[:], ident[:])
+        def q(c, lo, hi):
+            quantize("x%d" % c, lo, hi)
+
         neg_bias = sb.tile([P, N_TILES], F32, name="neg_bias")
-        nc.vector.tensor_scalar(
-            out=neg_bias[:], in0=bias_ps[:, 0:N_TILES], scalar1=-1.0, scalar2=None, op0=ALU.mult
-        )
+
+        def bias():
+            bias_ps = ps.tile([P, CHUNK], F32, name="bias_ps", tag="tanh%d" % (TANH_BANKS - 1))
+            nc.tensor.transpose(bias_ps[:, 0:P], bias_rows[:], ident[:])
+            nc.vector.tensor_scalar(
+                out=neg_bias[:], in0=bias_ps[:, 0:N_TILES], scalar1=-1.0, scalar2=None, op0=ALU.mult
+            )
 
         out_sb = [sb.tile([P, T], F32, name="out%d" % j) for j in range(N_TILES)]
         tanh_t = {}
@@ -136,16 +141,43 @@ def tile_mix_hway_tanh_none_kernel(tc, x, wg_words, wg_scales, wh, bg, res, out)
         diff = {}
         kept = {}
 
-        def products(u):
+        ga = {}
+        ha = {}
+
+        def mga(u):
+            c, j = divmod(u, N_TILES)
+            key = "x%d" % c
+            ga[u] = ps.tile([P, CHUNK], F32, name="ga%d" % u, tag="ga%d" % (u % 2))
+            nc.tensor.matmul_mx(
+                out=ga[u][:],
+                lhsT=wg_codes[:, j * P * PACK:(j + 1) * P * PACK].bitcast(FP8X4),
+                lhsT_scale=wg_plane[:, j * P:(j + 1) * P],
+                rhs=codes[key][:].bitcast(FP8X4),
+                rhs_scale=scales[key][:],
+                start=True,
+                stop=True,
+            )
+
+        def mha(u):
             c, j = divmod(u, N_TILES)
             key = "x%d" % c
             n_cols = slice(j * P, (j + 1) * P)
-            ga = ps.tile([P, CHUNK], F32, name="ga%d" % u, tag="ga%d" % (u % 2))
-            ha = ps.tile([P, CHUNK], F32, name="ha%d" % u, tag="ha%d" % (u % 2))
+            ha[u] = ps.tile([P, CHUNK], F32, name="ha%d" % u, tag="ha%d" % (u % 2))
+            if u in DIRECT:
+                nc.tensor.matmul_mx(
+                    out=ha[u][:],
+                    lhsT=codes["wh"][:, n_cols].bitcast(FP8X4),
+                    lhsT_scale=scales["wh"][:, n_cols],
+                    rhs=codes[key][:].bitcast(FP8X4),
+                    rhs_scale=scales[key][:],
+                    start=True,
+                    stop=True,
+                )
+                return
             for b in range(CHUNK // P):
                 t_cols = slice(b * P, (b + 1) * P)
                 nc.tensor.matmul_mx(
-                    out=ha[:, t_cols],
+                    out=ha[u][:, t_cols],
                     lhsT=codes[key][:, t_cols].bitcast(FP8X4),
                     lhsT_scale=scales[key][:, t_cols],
                     rhs=codes["wh"][:, n_cols].bitcast(FP8X4),
@@ -153,21 +185,27 @@ def tile_mix_hway_tanh_none_kernel(tc, x, wg_words, wg_scales, wh, bg, res, out)
                     start=True,
                     stop=True,
                 )
-            nc.tensor.matmul_mx(
-                out=ga[:],
-                lhsT=wg_codes[:, j * P * PACK:(j + 1) * P * PACK].bitcast(FP8X4),
-                lhsT_scale=wg_plane[:, n_cols],
-                rhs=codes[key][:].bitcast(FP8X4),
-                rhs_scale=scales[key][:],
-                start=True,
-                stop=True,
-            )
-            tanh_t[u] = sb.tile([P, CHUNK], F32, name="tanh_t%d" % u)
+
+        def sig(u):
+            j = u % N_TILES
             carry[u] = sb.tile([P, CHUNK], F32, name="carry%d" % u)
-            nc.scalar.activation(out=tanh_t[u][:], in_=ha[:], func=ACT.Tanh)
-            nc.scalar.activation(out=carry[u][:], in_=ga[:], func=ACT.Sigmoid, bias=neg_bias[:, j:j + 1], scale=-1.0)
+            nc.scalar.activation(out=carry[u][:], in_=ga[u][:], func=ACT.Sigmoid, bias=neg_bias[:, j:j + 1], scale=-1.0)
+
+        def th(u):
+            tanh_t[u] = sb.tile([P, CHUNK], F32, name="tanh_t%d" % u)
+            nc.scalar.activation(out=tanh_t[u][:], in_=ha[u][:], func=ACT.Tanh)
+            if u in DIRECT:
+                tanh_ps[u] = tanh_t[u]
+
+        def products(u):
+            mha(u)
+            mga(u)
+            th(u)
+            sig(u)
 
         def turn(u):
+            if u in DIRECT:
+                return
             tanh_ps[u] = ps.tile([P, CHUNK], F32, name="tanh_ps%d" % u, tag="tanh%d" % (u % TANH_BANKS))
             for b in range(CHUNK // P):
                 cols = slice(b * P, (b + 1) * P)
@@ -177,68 +215,82 @@ def tile_mix_hway_tanh_none_kernel(tc, x, wg_words, wg_scales, wh, bg, res, out)
             diff[u] = sb.tile([P, CHUNK], F32, name="diff%d" % u)
             nc.vector.tensor_tensor(out=diff[u][:], in0=tanh_ps[u][:], in1=res_sb[u][:], op=ALU.subtract)
 
-        def gate(u):
-            kept[u] = sb.tile([P, CHUNK], F32, name="kept%d" % u)
-            engine = nc.vector if u in VECTOR_GATED else nc.gpsimd
-            engine.tensor_tensor(out=kept[u][:], in0=diff[u][:], in1=carry[u][:], op=ALU.mult)
+        def gate(u, lo=0, hi=CHUNK, on_vector=False):
+            if lo == 0:
+                kept[u] = sb.tile([P, CHUNK], F32, name="kept%d" % u)
+            engine = nc.vector if (u in VECTOR_GATED or on_vector) else nc.gpsimd
+            engine.tensor_tensor(out=kept[u][:, lo:hi], in0=diff[u][:, lo:hi], in1=carry[u][:, lo:hi], op=ALU.mult)
 
-        def blend(u):
+        def blend(u, lo=0, hi=CHUNK):
             c, j = divmod(u, N_TILES)
             nc.vector.tensor_tensor(
-                out=out_sb[j][:, c * CHUNK:(c + 1) * CHUNK], in0=tanh_ps[u][:], in1=kept[u][:], op=ALU.subtract
+                out=out_sb[j][:, c * CHUNK + lo:c * CHUNK + hi],
+                in0=tanh_ps[u][:, lo:hi],
+                in1=kept[u][:, lo:hi],
+                op=ALU.subtract,
             )
 
-        products(0)
-        products(1)
-        interleave("wh", wh_raw[1][:], 1, False)
-        quantize("wh", 1)
-        turn(0)
-        subtract(0)
-        gate(0)
-        products(2)
-        turn(1)
-        subtract(1)
-        gate(1)
-        blend(0)
-        products(3)
-        interleave_x(1, 1, True)
-        blend(1)
-        interleave_x(1, 0, False)
-        quantize("x1", 0)
-        turn(2)
-        turn(3)
-        quantize("x1", 1)
-        products(4)
-        subtract(2)
-        gate(2)
-        subtract(3)
-        gate(3)
-        products(5)
-        blend(2)
-        for u in range(4, UNITS):
-            turn(u)
-            subtract(u)
-            if u not in VECTOR_GATED:
-                gate(u)
-            if u == 4:
-                blend(3)
-                interleave_x(2, 0, False)
-                interleave_x(2, 1, True)
-            if u == 5:
-                quantize("x2", 0)
-            if u >= 4 + BLEND_LAG:
-                blend(u - BLEND_LAG)
-            if u == 6:
-                quantize("x2", 1)
-            if u + 2 < UNITS:
-                products(u + 2)
-            if u in VECTOR_GATED:
-                gate(u)
-        for u in range(UNITS - BLEND_LAG, UNITS):
-            blend(u)
+        def store(j, lo, hi):
+            nc.sync.dma_start(out=out[j * P:(j + 1) * P, lo:hi], in_=out_sb[j][:, lo:hi])
 
-        first = (CHUNKS - 1) * CHUNK
-        for j in range(N_TILES):
-            nc.sync.dma_start(out=out[j * P:(j + 1) * P, 0:first], in_=out_sb[j][:, 0:first])
-        for j in range(N_TILES):
-            nc.sync.dma_start(out=out[j * P:(j + 1) * P, first:T], in_=out_sb[j][:, first:T])
+        il(0, 0, 256, False)
+        il(0, 256, 512, True)
+        q(0, 0, 256)
+        bias()
+        q(0, 256, 512)
+        for u in range(4):
+            mga(u)
+            sig(u)
+        interleave("wh", wh_raw[0], 0, 256, False)
+        interleave("wh", wh_raw[0], 256, 512, False)
+        quantize("wh", 0, 256)
+        quantize("wh", 256, 512)
+        il(1, 0, 256, False)
+        mha(0)
+        th(0)
+        mha(1)
+        th(1)
+        il(1, 256, 512, False)
+        q(1, 0, 256)
+        q(1, 256, 512)
+        for u in range(UNITS):
+            if True:
+                turn(u)
+            if u + 2 < UNITS:
+                mha(u + 2)
+                if u + 2 >= 4:
+                    mga(u + 2)
+            if not True:
+                turn(u)
+            if u + 2 < UNITS:
+                th(u + 2)
+                if u + 2 >= 4:
+                    sig(u + 2)
+            if u == 1:
+                il(2, 0, 256, True)
+            if u == 2:
+                il(2, 256, 512, True)
+            subtract(u)
+            if u not in VECTOR_GATED and u < 11:
+                gate(u)
+            if u - 1 in VECTOR_GATED:
+                gate(u - 1)
+            if u == 0 and False:
+                q(1, 256, 512)
+            if u == 3:
+                q(2, 0, 256)
+            if u == 4:
+                q(2, 256, 512)
+            if u >= 2:
+                blend(u - 2)
+        gate(11, 0, 256)
+        blend(10)
+        gate(11, 256, 512, True)
+        blend(11, 0, 256)
+        blend(11, 256, 512)
+        for j in range(4):
+            store(j, 0, 1024)
+        for j in range(3):
+            store(j, 1024, 1536)
+        store(3, 1024, 1280)
+        store(3, 1280, 1536)

@@ -17,15 +17,12 @@ ALU = mybir.AluOpType
 
 P = 128
 PACK = 4
-CHUNK = 512
-HALF = 256
+BANK = 512
 N_TILES = N // P
-CHUNKS = T // CHUNK
-UNITS = CHUNKS * N_TILES
-BLEND_LAG = 2
 TANH_BANKS = 4
-VECTOR_GATED = ()
-DIRECT = ()
+X_STARTS = (0, 512, 1024, 1536)
+TILES = tuple((c, j) for c in range(3) for j in range(4))
+VECTOR_GATED = (1, 8)
 
 
 def tile_mix_hway_tanh_none_kernel(tc, x, wg_words, wg_scales, wh, bg, res, out):
@@ -42,23 +39,28 @@ def tile_mix_hway_tanh_none_kernel(tc, x, wg_words, wg_scales, wh, bg, res, out)
         bias_rows = sb.tile([P, P], F32, name="bias_rows")
         nc.vector.memset(bias_rows[:], 0.0)
 
-        warm = sb.tile([P, 1], F32, name="warm")
-        nc.scalar.activation(out=warm[:], in_=ident[:, 0:1], func=ACT.Sigmoid)
+        def shape(u):
+            c, j0 = TILES[u]
+            width = X_STARTS[c + 1] - X_STARTS[c]
+            return c, j0, BANK // width, width
 
-        x_raw = {}
+        def hbm_tile(tensor, u):
+            c, j0, rows, width = shape(u)
+            return tensor.rearrange("(j p) t -> p j t", p=P)[:, j0:j0 + rows, X_STARTS[c]:X_STARTS[c + 1]]
+
+        raw = {}
         res_sb = {}
 
         def load_x(c):
-            x_raw[c] = sb.tile([P, PACK, CHUNK], F32, name="x_raw%d" % c)
+            raw[c] = sb.tile([P, PACK, X_STARTS[c + 1] - X_STARTS[c]], F32, name="x_raw%d" % c)
             nc.sync.dma_start(
-                out=x_raw[c][:],
-                in_=x.rearrange("(p j) t -> p j t", j=PACK)[:, :, c * CHUNK:(c + 1) * CHUNK],
+                out=raw[c][:], in_=x.rearrange("(p j) t -> p j t", j=PACK)[:, :, X_STARTS[c]:X_STARTS[c + 1]]
             )
 
         def load_res(u):
-            c, j = divmod(u, N_TILES)
-            res_sb[u] = sb.tile([P, CHUNK], F32, name="res%d" % u)
-            nc.sync.dma_start(out=res_sb[u][:], in_=res[j * P:(j + 1) * P, c * CHUNK:(c + 1) * CHUNK])
+            c, j0, rows, width = shape(u)
+            res_sb[u] = sb.tile([P, BANK], F32, name="res%d" % u)
+            nc.sync.dma_start(out=res_sb[u][:].rearrange("p (j t) -> p j t", j=rows), in_=hbm_tile(res, u))
 
         wh_raw = {}
 
@@ -86,8 +88,8 @@ def tile_mix_hway_tanh_none_kernel(tc, x, wg_words, wg_scales, wh, bg, res, out)
         load_x(1)
         load_res(0)
         load_res(1)
-        load_x(2)
         load_res(2)
+        load_x(2)
         load_res(3)
         load_res(4)
         load_res(5)
@@ -101,85 +103,74 @@ def tile_mix_hway_tanh_none_kernel(tc, x, wg_words, wg_scales, wh, bg, res, out)
         grouped = {}
         codes = {}
         scales = {}
-        for key in ("x0", "x1", "x2", "wh"):
-            codes[key] = sb.tile([P, CHUNK], U32, name="codes_%s" % key, align_bytes=64)
-            scales[key] = sb.tile([P, CHUNK], U8, name="scales_%s" % key, align_bytes=64)
+        for key in list(range(len(X_STARTS) - 1)) + ["wh"]:
+            cols = N if key == "wh" else X_STARTS[key + 1] - X_STARTS[key]
+            codes[key] = sb.tile([P, cols], U32, name="codes_%s" % key, align_bytes=64)
+            scales[key] = sb.tile([P, cols], U8, name="scales_%s" % key, align_bytes=64)
 
-        def interleave(key, raw, lo, hi, on_scalar, base=0):
+        def interleave(key, source, lo, hi, on_scalar, base=0):
             grouped[key, lo] = sb.tile([P, (hi - lo) * PACK], BF16, name="grouped_%s_%d" % (key, lo), align_bytes=64)
             dst = grouped[key, lo][:].rearrange("p (c i j) -> p c j i", i=4, j=PACK)
-            src = raw[:, :, lo - base:hi - base].rearrange("p j (c i) -> p c j i", i=4)
+            src = source[:, :, lo - base:hi - base].rearrange("p j (c i) -> p c j i", i=4)
             if on_scalar:
                 nc.scalar.copy(out=dst, in_=src)
             else:
                 nc.vector.tensor_copy(out=dst, in_=src)
 
-        def quantize(key, lo, hi):
+        def q(key, lo, hi):
             nc.vector.quantize_mx(
                 out=codes[key][:, lo:hi].bitcast(FP8X4), scales=scales[key][:, lo:hi], in_=grouped[key, lo][:]
             )
 
         def il(c, lo, hi, on_scalar):
-            interleave("x%d" % c, x_raw[c], lo, hi, on_scalar)
+            interleave(c, raw[c], lo, hi, on_scalar)
 
-        def q(c, lo, hi):
-            quantize("x%d" % c, lo, hi)
+        def ilw(lo, hi, on_scalar, base=0):
+            interleave("wh", wh_raw[base], lo, hi, on_scalar, base)
 
         neg_bias = sb.tile([P, N_TILES], F32, name="neg_bias")
 
         def bias():
-            bias_ps = ps.tile([P, CHUNK], F32, name="bias_ps", tag="tanh%d" % (TANH_BANKS - 1))
+            bias_ps = ps.tile([P, BANK], F32, name="bias_ps", tag="tanh%d" % (TANH_BANKS - 1))
             nc.tensor.transpose(bias_ps[:, 0:P], bias_rows[:], ident[:])
             nc.vector.tensor_scalar(
                 out=neg_bias[:], in0=bias_ps[:, 0:N_TILES], scalar1=-1.0, scalar2=None, op0=ALU.mult
             )
 
-        out_sb = [sb.tile([P, T], F32, name="out%d" % j) for j in range(N_TILES)]
         tanh_t = {}
         carry = {}
         tanh_ps = {}
         diff = {}
         kept = {}
-
+        out_sb = {}
         ga = {}
         ha = {}
 
         def mga(u):
-            c, j = divmod(u, N_TILES)
-            key = "x%d" % c
-            ga[u] = ps.tile([P, CHUNK], F32, name="ga%d" % u, tag="ga%d" % (u % 2))
-            nc.tensor.matmul_mx(
-                out=ga[u][:],
-                lhsT=wg_codes[:, j * P * PACK:(j + 1) * P * PACK].bitcast(FP8X4),
-                lhsT_scale=wg_plane[:, j * P:(j + 1) * P],
-                rhs=codes[key][:].bitcast(FP8X4),
-                rhs_scale=scales[key][:],
-                start=True,
-                stop=True,
-            )
-
-        def mha(u):
-            c, j = divmod(u, N_TILES)
-            key = "x%d" % c
-            n_cols = slice(j * P, (j + 1) * P)
-            ha[u] = ps.tile([P, CHUNK], F32, name="ha%d" % u, tag="ha%d" % (u % 2))
-            if u in DIRECT:
+            c, j0, rows, width = shape(u)
+            ga[u] = ps.tile([P, BANK], F32, name="ga%d" % u, tag="ga%d" % (u % 2))
+            for r in range(rows):
+                j = j0 + r
                 nc.tensor.matmul_mx(
-                    out=ha[u][:],
-                    lhsT=codes["wh"][:, n_cols].bitcast(FP8X4),
-                    lhsT_scale=scales["wh"][:, n_cols],
-                    rhs=codes[key][:].bitcast(FP8X4),
-                    rhs_scale=scales[key][:],
+                    out=ga[u][:, r * width:(r + 1) * width],
+                    lhsT=wg_codes[:, j * P * PACK:(j + 1) * P * PACK].bitcast(FP8X4),
+                    lhsT_scale=wg_plane[:, j * P:(j + 1) * P],
+                    rhs=codes[c][:].bitcast(FP8X4),
+                    rhs_scale=scales[c][:],
                     start=True,
                     stop=True,
                 )
-                return
-            for b in range(CHUNK // P):
+
+        def mha(u):
+            c, j0, rows, width = shape(u)
+            n_cols = slice(j0 * P, (j0 + rows) * P)
+            ha[u] = ps.tile([P, BANK], F32, name="ha%d" % u, tag="ha%d" % (u % 2))
+            for b in range(width // P):
                 t_cols = slice(b * P, (b + 1) * P)
                 nc.tensor.matmul_mx(
-                    out=ha[u][:, t_cols],
-                    lhsT=codes[key][:, t_cols].bitcast(FP8X4),
-                    lhsT_scale=scales[key][:, t_cols],
+                    out=ha[u][:, b * rows * P:(b + 1) * rows * P],
+                    lhsT=codes[c][:, t_cols].bitcast(FP8X4),
+                    lhsT_scale=scales[c][:, t_cols],
                     rhs=codes["wh"][:, n_cols].bitcast(FP8X4),
                     rhs_scale=scales["wh"][:, n_cols],
                     start=True,
@@ -187,110 +178,112 @@ def tile_mix_hway_tanh_none_kernel(tc, x, wg_words, wg_scales, wh, bg, res, out)
                 )
 
         def sig(u):
-            j = u % N_TILES
-            carry[u] = sb.tile([P, CHUNK], F32, name="carry%d" % u)
-            nc.scalar.activation(out=carry[u][:], in_=ga[u][:], func=ACT.Sigmoid, bias=neg_bias[:, j:j + 1], scale=-1.0)
+            c, j0, rows, width = shape(u)
+            carry[u] = sb.tile([P, BANK], F32, name="carry%d" % u)
+            for r in range(rows):
+                cols = slice(r * width, (r + 1) * width)
+                nc.scalar.activation(
+                    out=carry[u][:, cols], in_=ga[u][:, cols], func=ACT.Sigmoid,
+                    bias=neg_bias[:, j0 + r:j0 + r + 1], scale=-1.0,
+                )
 
         def th(u):
-            tanh_t[u] = sb.tile([P, CHUNK], F32, name="tanh_t%d" % u)
+            tanh_t[u] = sb.tile([P, BANK], F32, name="tanh_t%d" % u)
             nc.scalar.activation(out=tanh_t[u][:], in_=ha[u][:], func=ACT.Tanh)
-            if u in DIRECT:
-                tanh_ps[u] = tanh_t[u]
-
-        def products(u):
-            mha(u)
-            mga(u)
-            th(u)
-            sig(u)
 
         def turn(u):
-            if u in DIRECT:
-                return
-            tanh_ps[u] = ps.tile([P, CHUNK], F32, name="tanh_ps%d" % u, tag="tanh%d" % (u % TANH_BANKS))
-            for b in range(CHUNK // P):
-                cols = slice(b * P, (b + 1) * P)
-                nc.tensor.transpose(tanh_ps[u][:, cols], tanh_t[u][:, cols], ident[:])
+            c, j0, rows, width = shape(u)
+            tanh_ps[u] = ps.tile([P, BANK], F32, name="tanh_ps%d" % u, tag="tanh%d" % (u % TANH_BANKS))
+            for r in range(rows):
+                for b in range(width // P):
+                    src = (b * rows + r) * P
+                    dst = r * width + b * P
+                    nc.tensor.transpose(tanh_ps[u][:, dst:dst + P], tanh_t[u][:, src:src + P], ident[:])
 
         def subtract(u):
-            diff[u] = sb.tile([P, CHUNK], F32, name="diff%d" % u)
+            diff[u] = sb.tile([P, BANK], F32, name="diff%d" % u)
             nc.vector.tensor_tensor(out=diff[u][:], in0=tanh_ps[u][:], in1=res_sb[u][:], op=ALU.subtract)
 
-        def gate(u, lo=0, hi=CHUNK, on_vector=False):
+        def gate(u, lo=0, hi=BANK, on_vector=False):
             if lo == 0:
-                kept[u] = sb.tile([P, CHUNK], F32, name="kept%d" % u)
+                kept[u] = sb.tile([P, BANK], F32, name="kept%d" % u)
             engine = nc.vector if (u in VECTOR_GATED or on_vector) else nc.gpsimd
             engine.tensor_tensor(out=kept[u][:, lo:hi], in0=diff[u][:, lo:hi], in1=carry[u][:, lo:hi], op=ALU.mult)
 
-        def blend(u, lo=0, hi=CHUNK):
-            c, j = divmod(u, N_TILES)
+        def blend(u, lo=0, hi=BANK):
+            if lo == 0:
+                out_sb[u] = sb.tile([P, BANK], F32, name="out%d" % u)
             nc.vector.tensor_tensor(
-                out=out_sb[j][:, c * CHUNK + lo:c * CHUNK + hi],
-                in0=tanh_ps[u][:, lo:hi],
-                in1=kept[u][:, lo:hi],
-                op=ALU.subtract,
+                out=out_sb[u][:, lo:hi], in0=tanh_ps[u][:, lo:hi], in1=kept[u][:, lo:hi], op=ALU.subtract
             )
 
-        def store(j, lo, hi):
-            nc.sync.dma_start(out=out[j * P:(j + 1) * P, lo:hi], in_=out_sb[j][:, lo:hi])
+        def store(u):
+            c, j0, rows, width = shape(u)
+            nc.sync.dma_start(out=hbm_tile(out, u), in_=out_sb[u][:].rearrange("p (j t) -> p j t", j=rows))
+
+        def store_part(u, lo, hi):
+            nc.sync.dma_start(out=hbm_tile(out, u)[:, 0, lo:hi], in_=out_sb[u][:, lo:hi])
 
         il(0, 0, 256, False)
-        il(0, 256, 512, True)
+        il(0, 256, 512, False)
         q(0, 0, 256)
-        bias()
         q(0, 256, 512)
-        for u in range(4):
+        bias()
+        for u in range(3):
             mga(u)
             sig(u)
-        interleave("wh", wh_raw[0], 0, 256, False)
-        interleave("wh", wh_raw[0], 256, 512, False)
-        quantize("wh", 0, 256)
-        quantize("wh", 256, 512)
-        il(1, 0, 256, False)
+        ilw(0, 256, False)
+        ilw(256, 512, False)
+        q("wh", 0, 256)
+        q("wh", 256, 512)
         mha(0)
         th(0)
+        il(1, 0, 256, False)
+        il(1, 256, 512, False)
         mha(1)
         th(1)
-        il(1, 256, 512, False)
         q(1, 0, 256)
         q(1, 256, 512)
-        for u in range(UNITS):
+        for u in range(3, 4):
+            mga(u)
+            sig(u)
+        for u in range(12):
             if True:
                 turn(u)
-            if u + 2 < UNITS:
+            if u + 2 < 12:
                 mha(u + 2)
-                if u + 2 >= 4:
-                    mga(u + 2)
-            if not True:
+            if 4 <= u + 1 < 12:
+                mga(u + 1)
+            if not (True):
                 turn(u)
-            if u + 2 < UNITS:
+            if u + 2 < 12:
                 th(u + 2)
-                if u + 2 >= 4:
-                    sig(u + 2)
-            if u == 1:
-                il(2, 0, 256, True)
+            if 4 <= u + 1 < 12:
+                sig(u + 1)
             if u == 2:
+                il(2, 0, 256, True)
+            if u == 3:
                 il(2, 256, 512, True)
+            if u == 0 and False:
+                q(1, 256, 512)
             subtract(u)
             if u not in VECTOR_GATED and u < 11:
                 gate(u)
             if u - 1 in VECTOR_GATED:
                 gate(u - 1)
-            if u == 0 and False:
-                q(1, 256, 512)
-            if u == 3:
-                q(2, 0, 256)
             if u == 4:
+                q(2, 0, 256)
+            if u == 5:
                 q(2, 256, 512)
             if u >= 2:
                 blend(u - 2)
+
         gate(11, 0, 256)
         blend(10)
         gate(11, 256, 512, True)
         blend(11, 0, 256)
         blend(11, 256, 512)
-        for j in range(4):
-            store(j, 0, 1024)
-        for j in range(3):
-            store(j, 1024, 1536)
-        store(3, 1024, 1280)
-        store(3, 1280, 1536)
+        for u in range(11):
+            store(u)
+        store_part(11, 0, 256)
+        store_part(11, 256, 512)

@@ -17,12 +17,24 @@ ALU = mybir.AluOpType
 
 P = 128
 PACK = 4
-BANK = 512
-N_TILES = N // P
-TANH_BANKS = 4
-X_STARTS = (0, 512, 1024, 1536)
-TILES = tuple((c, j) for c in range(3) for j in range(4))
-VECTOR_GATED = (1, 8)
+LINE = 4
+WIDTH = 512
+HALF = WIDTH // 2
+GROUPS = N // P
+CHUNKS = T // WIDTH
+TILES = CHUNKS * GROUPS
+LAST = TILES - 1
+
+SUM_BANKS = 2
+H_BANKS = 4
+
+TANH_LEAD = 2
+CARRY_LEAD = 1
+BLEND_LAG = 2
+
+EARLY_RES = 3
+LAST_CHUNK_STEP = 2
+VECTOR_PRODUCTS = (1,)
 
 
 def tile_mix_hway_tanh_none_kernel(tc, x, wg_words, wg_scales, wh, bg, res, out):
@@ -34,256 +46,197 @@ def tile_mix_hway_tanh_none_kernel(tc, x, wg_words, wg_scales, wh, bg, res, out)
 
         ident = sb.tile([P, P], F32, name="ident")
         make_identity(nc, ident[:])
-        wg_plane = sb.tile([P, N], U8, name="wg_plane", align_bytes=64)
-        nc.vector.memset(wg_plane[:].bitcast(U32), 0)
+        wg_scale_sb = sb.tile([P, N], U8, name="wg_scale_sb", align_bytes=64)
+        nc.vector.memset(wg_scale_sb[:].bitcast(U32), 0)
         bias_rows = sb.tile([P, P], F32, name="bias_rows")
         nc.vector.memset(bias_rows[:], 0.0)
 
-        def shape(u):
-            c, j0 = TILES[u]
-            width = X_STARTS[c + 1] - X_STARTS[c]
-            return c, j0, BANK // width, width
+        def tokens(chunk):
+            return slice(chunk * WIDTH, (chunk + 1) * WIDTH)
 
-        def hbm_tile(tensor, u):
-            c, j0, rows, width = shape(u)
-            return tensor.rearrange("(j p) t -> p j t", p=P)[:, j0:j0 + rows, X_STARTS[c]:X_STARTS[c + 1]]
+        def features(u):
+            return slice(u % GROUPS * P, (u % GROUPS + 1) * P)
 
         raw = {}
         res_sb = {}
 
-        def load_x(c):
-            raw[c] = sb.tile([P, PACK, X_STARTS[c + 1] - X_STARTS[c]], F32, name="x_raw%d" % c)
-            nc.sync.dma_start(
-                out=raw[c][:], in_=x.rearrange("(p j) t -> p j t", j=PACK)[:, :, X_STARTS[c]:X_STARTS[c + 1]]
-            )
+        def load_x(chunk):
+            raw[chunk] = sb.tile([P, PACK, WIDTH], F32, name="x_raw%d" % chunk)
+            nc.sync.dma_start(out=raw[chunk][:], in_=x.rearrange("(p i) t -> p i t", i=PACK)[:, :, tokens(chunk)])
 
         def load_res(u):
-            c, j0, rows, width = shape(u)
-            res_sb[u] = sb.tile([P, BANK], F32, name="res%d" % u)
-            nc.sync.dma_start(out=res_sb[u][:].rearrange("p (j t) -> p j t", j=rows), in_=hbm_tile(res, u))
-
-        wh_raw = {}
-
-        def load_wh(lo, hi):
-            wh_raw[lo] = sb.tile([P, PACK, hi - lo], F32, name="wh_raw%d" % lo)
-            nc.sync.dma_start(out=wh_raw[lo][:], in_=wh.rearrange("(p j) n -> p j n", j=PACK)[:, :, lo:hi])
+            res_sb[u] = sb.tile([P, WIDTH], F32, name="res%d" % u)
+            nc.sync.dma_start(out=res_sb[u][:], in_=res[features(u), tokens(u // GROUPS)])
 
         wg_codes = sb.tile([P, N * PACK], U8, name="wg_codes", align_bytes=64)
-
-        def load_wg():
-            nc.sync.dma_start(out=bias_rows[0:N_TILES, :], in_=bg.rearrange("(j p) -> j p", p=P))
-            for q in range(4):
-                nc.sync.dma_start(
-                    out=wg_plane[32 * q:32 * q + 4, :].bitcast(I32),
-                    in_=wg_scales[0, 4 * q:4 * q + 4, :].bitcast(I32),
-                )
-            nc.sync.dma_start(
-                out=wg_codes[:].bitcast(I32),
-                in_=wg_words[0].rearrange("p n t -> p (n t)").bitcast(I32),
-            )
-
         load_x(0)
-        load_wg()
-        load_wh(0, 512)
+        nc.sync.dma_start(out=bias_rows[0:GROUPS, :], in_=bg.rearrange("(g p) -> g p", p=P))
+        for s in range(4):
+            nc.sync.dma_start(
+                out=wg_scale_sb[32 * s:32 * s + 4, :].bitcast(I32),
+                in_=wg_scales[0, 4 * s:4 * s + 4, :].bitcast(I32),
+            )
+        nc.sync.dma_start(
+            out=wg_codes[:].bitcast(I32),
+            in_=wg_words[0].rearrange("p n i -> p (n i)").bitcast(I32),
+        )
+        raw["wh"] = sb.tile([P, PACK, N], F32, name="wh_raw")
+        nc.sync.dma_start(out=raw["wh"][:], in_=wh.rearrange("(p i) n -> p i n", i=PACK))
         load_x(1)
-        load_res(0)
-        load_res(1)
-        load_res(2)
-        load_x(2)
-        load_res(3)
-        load_res(4)
-        load_res(5)
-        load_res(6)
-        load_res(7)
-        load_res(8)
-        load_res(9)
-        load_res(10)
-        load_res(11)
+        for u in range(EARLY_RES):
+            load_res(u)
+        load_x(CHUNKS - 1)
+        for u in range(EARLY_RES, TILES):
+            load_res(u)
 
         grouped = {}
         codes = {}
         scales = {}
-        for key in list(range(len(X_STARTS) - 1)) + ["wh"]:
-            cols = N if key == "wh" else X_STARTS[key + 1] - X_STARTS[key]
-            codes[key] = sb.tile([P, cols], U32, name="codes_%s" % key, align_bytes=64)
-            scales[key] = sb.tile([P, cols], U8, name="scales_%s" % key, align_bytes=64)
+        for key in list(range(CHUNKS)) + ["wh"]:
+            codes[key] = sb.tile([P, WIDTH], U32, name="codes_%s" % key, align_bytes=64)
+            scales[key] = sb.tile([P, WIDTH], U8, name="scales_%s" % key, align_bytes=64)
 
-        def interleave(key, source, lo, hi, on_scalar, base=0):
-            grouped[key, lo] = sb.tile([P, (hi - lo) * PACK], BF16, name="grouped_%s_%d" % (key, lo), align_bytes=64)
-            dst = grouped[key, lo][:].rearrange("p (c i j) -> p c j i", i=4, j=PACK)
-            src = source[:, :, lo - base:hi - base].rearrange("p j (c i) -> p c j i", i=4)
-            if on_scalar:
-                nc.scalar.copy(out=dst, in_=src)
-            else:
-                nc.vector.tensor_copy(out=dst, in_=src)
+        def interleave(copy, key, half):
+            grouped[key, half] = sb.tile(
+                [P, HALF * PACK], BF16, name="grouped_%s_%d" % (key, half), align_bytes=64
+            )
+            copy(
+                out=grouped[key, half][:].rearrange("p (c e i) -> p c i e", e=LINE, i=PACK),
+                in_=raw[key][:, :, half * HALF:(half + 1) * HALF].rearrange("p i (c e) -> p c i e", e=LINE),
+            )
 
-        def q(key, lo, hi):
+        def quantize(key, half):
+            cols = slice(half * HALF, (half + 1) * HALF)
             nc.vector.quantize_mx(
-                out=codes[key][:, lo:hi].bitcast(FP8X4), scales=scales[key][:, lo:hi], in_=grouped[key, lo][:]
+                out=codes[key][:, cols].bitcast(FP8X4), scales=scales[key][:, cols], in_=grouped[key, half][:]
             )
 
-        def il(c, lo, hi, on_scalar):
-            interleave(c, raw[c], lo, hi, on_scalar)
+        def quantize_on_vector(key):
+            for half in range(2):
+                interleave(nc.vector.tensor_copy, key, half)
+            for half in range(2):
+                quantize(key, half)
 
-        def ilw(lo, hi, on_scalar, base=0):
-            interleave("wh", wh_raw[base], lo, hi, on_scalar, base)
-
-        neg_bias = sb.tile([P, N_TILES], F32, name="neg_bias")
-
-        def bias():
-            bias_ps = ps.tile([P, BANK], F32, name="bias_ps", tag="tanh%d" % (TANH_BANKS - 1))
-            nc.tensor.transpose(bias_ps[:, 0:P], bias_rows[:], ident[:])
-            nc.vector.tensor_scalar(
-                out=neg_bias[:], in0=bias_ps[:, 0:N_TILES], scalar1=-1.0, scalar2=None, op0=ALU.mult
-            )
-
-        tanh_t = {}
+        neg_bias = sb.tile([P, GROUPS], F32, name="neg_bias")
+        ga = {}
+        ha = {}
         carry = {}
-        tanh_ps = {}
+        h_by_token = {}
+        h_ps = {}
         diff = {}
         kept = {}
         out_sb = {}
-        ga = {}
-        ha = {}
 
-        def mga(u):
-            c, j0, rows, width = shape(u)
-            ga[u] = ps.tile([P, BANK], F32, name="ga%d" % u, tag="ga%d" % (u % 2))
-            for r in range(rows):
-                j = j0 + r
-                nc.tensor.matmul_mx(
-                    out=ga[u][:, r * width:(r + 1) * width],
-                    lhsT=wg_codes[:, j * P * PACK:(j + 1) * P * PACK].bitcast(FP8X4),
-                    lhsT_scale=wg_plane[:, j * P:(j + 1) * P],
-                    rhs=codes[c][:].bitcast(FP8X4),
-                    rhs_scale=scales[c][:],
-                    start=True,
-                    stop=True,
-                )
-
-        def mha(u):
-            c, j0, rows, width = shape(u)
-            n_cols = slice(j0 * P, (j0 + rows) * P)
-            ha[u] = ps.tile([P, BANK], F32, name="ha%d" % u, tag="ha%d" % (u % 2))
-            for b in range(width // P):
-                t_cols = slice(b * P, (b + 1) * P)
-                nc.tensor.matmul_mx(
-                    out=ha[u][:, b * rows * P:(b + 1) * rows * P],
-                    lhsT=codes[c][:, t_cols].bitcast(FP8X4),
-                    lhsT_scale=scales[c][:, t_cols],
-                    rhs=codes["wh"][:, n_cols].bitcast(FP8X4),
-                    rhs_scale=scales["wh"][:, n_cols],
-                    start=True,
-                    stop=True,
-                )
-
-        def sig(u):
-            c, j0, rows, width = shape(u)
-            carry[u] = sb.tile([P, BANK], F32, name="carry%d" % u)
-            for r in range(rows):
-                cols = slice(r * width, (r + 1) * width)
-                nc.scalar.activation(
-                    out=carry[u][:, cols], in_=ga[u][:, cols], func=ACT.Sigmoid,
-                    bias=neg_bias[:, j0 + r:j0 + r + 1], scale=-1.0,
-                )
-
-        def th(u):
-            tanh_t[u] = sb.tile([P, BANK], F32, name="tanh_t%d" % u)
-            nc.scalar.activation(out=tanh_t[u][:], in_=ha[u][:], func=ACT.Tanh)
-
-        def turn(u):
-            c, j0, rows, width = shape(u)
-            tanh_ps[u] = ps.tile([P, BANK], F32, name="tanh_ps%d" % u, tag="tanh%d" % (u % TANH_BANKS))
-            for r in range(rows):
-                for b in range(width // P):
-                    src = (b * rows + r) * P
-                    dst = r * width + b * P
-                    nc.tensor.transpose(tanh_ps[u][:, dst:dst + P], tanh_t[u][:, src:src + P], ident[:])
-
-        def subtract(u):
-            diff[u] = sb.tile([P, BANK], F32, name="diff%d" % u)
-            nc.vector.tensor_tensor(out=diff[u][:], in0=tanh_ps[u][:], in1=res_sb[u][:], op=ALU.subtract)
-
-        def gate(u, lo=0, hi=BANK, on_vector=False):
-            if lo == 0:
-                kept[u] = sb.tile([P, BANK], F32, name="kept%d" % u)
-            engine = nc.vector if (u in VECTOR_GATED or on_vector) else nc.gpsimd
-            engine.tensor_tensor(out=kept[u][:, lo:hi], in0=diff[u][:, lo:hi], in1=carry[u][:, lo:hi], op=ALU.mult)
-
-        def blend(u, lo=0, hi=BANK):
-            if lo == 0:
-                out_sb[u] = sb.tile([P, BANK], F32, name="out%d" % u)
-            nc.vector.tensor_tensor(
-                out=out_sb[u][:, lo:hi], in0=tanh_ps[u][:, lo:hi], in1=kept[u][:, lo:hi], op=ALU.subtract
+        def gate_sum(u):
+            ga[u] = ps.tile([P, WIDTH], F32, name="ga%d" % u, tag="ga%d" % (u % SUM_BANKS))
+            group = u % GROUPS
+            nc.tensor.matmul_mx(
+                out=ga[u][:],
+                lhsT=wg_codes[:, group * P * PACK:(group + 1) * P * PACK].bitcast(FP8X4),
+                lhsT_scale=wg_scale_sb[:, features(u)],
+                rhs=codes[u // GROUPS][:].bitcast(FP8X4),
+                rhs_scale=scales[u // GROUPS][:],
+                start=True,
+                stop=True,
             )
 
-        def store(u):
-            c, j0, rows, width = shape(u)
-            nc.sync.dma_start(out=hbm_tile(out, u), in_=out_sb[u][:].rearrange("p (j t) -> p j t", j=rows))
+        def value_sum(u):
+            ha[u] = ps.tile([P, WIDTH], F32, name="ha%d" % u, tag="ha%d" % (u % SUM_BANKS))
+            for b in range(WIDTH // P):
+                block = slice(b * P, (b + 1) * P)
+                nc.tensor.matmul_mx(
+                    out=ha[u][:, block],
+                    lhsT=codes[u // GROUPS][:, block].bitcast(FP8X4),
+                    lhsT_scale=scales[u // GROUPS][:, block],
+                    rhs=codes["wh"][:, features(u)].bitcast(FP8X4),
+                    rhs_scale=scales["wh"][:, features(u)],
+                    start=True,
+                    stop=True,
+                )
 
-        def store_part(u, lo, hi):
-            nc.sync.dma_start(out=hbm_tile(out, u)[:, 0, lo:hi], in_=out_sb[u][:, lo:hi])
+        def sigmoid(u):
+            carry[u] = sb.tile([P, WIDTH], F32, name="carry%d" % u)
+            group = u % GROUPS
+            nc.scalar.activation(
+                out=carry[u][:], in_=ga[u][:], func=ACT.Sigmoid, bias=neg_bias[:, group:group + 1], scale=-1.0
+            )
 
-        il(0, 0, 256, False)
-        il(0, 256, 512, False)
-        q(0, 0, 256)
-        q(0, 256, 512)
-        bias()
-        for u in range(3):
-            mga(u)
-            sig(u)
-        ilw(0, 256, False)
-        ilw(256, 512, False)
-        q("wh", 0, 256)
-        q("wh", 256, 512)
-        mha(0)
-        th(0)
-        il(1, 0, 256, False)
-        il(1, 256, 512, False)
-        mha(1)
-        th(1)
-        q(1, 0, 256)
-        q(1, 256, 512)
-        for u in range(3, 4):
-            mga(u)
-            sig(u)
-        for u in range(12):
-            if True:
-                turn(u)
-            if u + 2 < 12:
-                mha(u + 2)
-            if 4 <= u + 1 < 12:
-                mga(u + 1)
-            if not (True):
-                turn(u)
-            if u + 2 < 12:
-                th(u + 2)
-            if 4 <= u + 1 < 12:
-                sig(u + 1)
-            if u == 2:
-                il(2, 0, 256, True)
-            if u == 3:
-                il(2, 256, 512, True)
-            if u == 0 and False:
-                q(1, 256, 512)
+        def tanh(u):
+            h_by_token[u] = sb.tile([P, WIDTH], F32, name="h_by_token%d" % u)
+            nc.scalar.activation(out=h_by_token[u][:], in_=ha[u][:], func=ACT.Tanh)
+
+        def turn(u):
+            h_ps[u] = ps.tile([P, WIDTH], F32, name="h_ps%d" % u, tag="h%d" % (u % H_BANKS))
+            for b in range(WIDTH // P):
+                block = slice(b * P, (b + 1) * P)
+                nc.tensor.transpose(h_ps[u][:, block], h_by_token[u][:, block], ident[:])
+
+        def subtract(u):
+            diff[u] = sb.tile([P, WIDTH], F32, name="diff%d" % u)
+            nc.vector.tensor_tensor(out=diff[u][:], in0=h_ps[u][:], in1=res_sb[u][:], op=ALU.subtract)
+
+        def multiply(engine, u, lo=0, hi=WIDTH):
+            if lo == 0:
+                kept[u] = sb.tile([P, WIDTH], F32, name="kept%d" % u)
+            engine.tensor_tensor(out=kept[u][:, lo:hi], in0=diff[u][:, lo:hi], in1=carry[u][:, lo:hi], op=ALU.mult)
+
+        def blend(u, lo=0, hi=WIDTH):
+            if lo == 0:
+                out_sb[u] = sb.tile([P, WIDTH], F32, name="out%d" % u)
+            nc.vector.tensor_tensor(
+                out=out_sb[u][:, lo:hi], in0=h_ps[u][:, lo:hi], in1=kept[u][:, lo:hi], op=ALU.subtract
+            )
+
+        def store(u, lo=0, hi=WIDTH):
+            nc.sync.dma_start(out=out[features(u), tokens(u // GROUPS)][:, lo:hi], in_=out_sb[u][:, lo:hi])
+
+        quantize_on_vector(0)
+        bias_ps = ps.tile([P, WIDTH], F32, name="bias_ps", tag="h%d" % (H_BANKS - 1))
+        nc.tensor.transpose(bias_ps[:, 0:P], bias_rows[:], ident[:])
+        nc.vector.tensor_scalar(out=neg_bias[:], in0=bias_ps[:, 0:GROUPS], scalar1=-1.0, scalar2=None, op0=ALU.mult)
+        for u in range(GROUPS - 1):
+            gate_sum(u)
+            sigmoid(u)
+        quantize_on_vector("wh")
+        for u in range(TANH_LEAD):
+            value_sum(u)
+            tanh(u)
+        quantize_on_vector(1)
+        gate_sum(GROUPS - 1)
+        sigmoid(GROUPS - 1)
+
+        for u in range(TILES):
+            turn(u)
+            makes_tanh = u + TANH_LEAD < TILES
+            makes_carry = GROUPS <= u + CARRY_LEAD < TILES
+            if makes_tanh:
+                value_sum(u + TANH_LEAD)
+            if makes_carry:
+                gate_sum(u + CARRY_LEAD)
+            if makes_tanh:
+                tanh(u + TANH_LEAD)
+            if makes_carry:
+                sigmoid(u + CARRY_LEAD)
+            if 0 <= u - LAST_CHUNK_STEP < 2:
+                interleave(nc.scalar.copy, CHUNKS - 1, u - LAST_CHUNK_STEP)
             subtract(u)
-            if u not in VECTOR_GATED and u < 11:
-                gate(u)
-            if u - 1 in VECTOR_GATED:
-                gate(u - 1)
-            if u == 4:
-                q(2, 0, 256)
-            if u == 5:
-                q(2, 256, 512)
-            if u >= 2:
-                blend(u - 2)
+            if u not in VECTOR_PRODUCTS and u != LAST:
+                multiply(nc.gpsimd, u)
+            if u - 1 in VECTOR_PRODUCTS:
+                multiply(nc.vector, u - 1)
+            if 2 <= u - LAST_CHUNK_STEP < 4:
+                quantize(CHUNKS - 1, u - LAST_CHUNK_STEP - 2)
+            if u >= BLEND_LAG:
+                blend(u - BLEND_LAG)
 
-        gate(11, 0, 256)
-        blend(10)
-        gate(11, 256, 512, True)
-        blend(11, 0, 256)
-        blend(11, 256, 512)
-        for u in range(11):
+        multiply(nc.gpsimd, LAST, 0, HALF)
+        for u in range(TILES - BLEND_LAG, LAST):
+            blend(u)
+        multiply(nc.vector, LAST, HALF, WIDTH)
+        blend(LAST, 0, HALF)
+        blend(LAST, HALF, WIDTH)
+
+        for u in range(LAST):
             store(u)
-        store_part(11, 0, 256)
-        store_part(11, 256, 512)
+        store(LAST, 0, HALF)
+        store(LAST, HALF, WIDTH)

@@ -24,6 +24,10 @@ GROUPS = N // P
 CHUNKS = T // WIDTH
 TILES = CHUNKS * GROUPS
 LAST = TILES - 1
+QUADRANT = 32
+SCALE_ROWS = 4
+
+assert CHUNKS == 3
 
 SUM_BANKS = 2
 H_BANKS = 4
@@ -34,7 +38,7 @@ BLEND_LAG = 2
 
 EARLY_RES = 3
 LAST_CHUNK_STEP = 2
-VECTOR_PRODUCTS = (1,)
+VECTOR_PRODUCTS = (1, 8)
 
 
 def tile_mix_hway_tanh_none_kernel(tc, x, wg_words, wg_scales, wh, bg, res, out):
@@ -71,10 +75,10 @@ def tile_mix_hway_tanh_none_kernel(tc, x, wg_words, wg_scales, wh, bg, res, out)
         wg_codes = sb.tile([P, N * PACK], U8, name="wg_codes", align_bytes=64)
         load_x(0)
         nc.sync.dma_start(out=bias_rows[0:GROUPS, :], in_=bg.rearrange("(g p) -> g p", p=P))
-        for s in range(4):
+        for s in range(P // QUADRANT):
             nc.sync.dma_start(
-                out=wg_scale_sb[32 * s:32 * s + 4, :].bitcast(I32),
-                in_=wg_scales[0, 4 * s:4 * s + 4, :].bitcast(I32),
+                out=wg_scale_sb[QUADRANT * s:QUADRANT * s + SCALE_ROWS, :].bitcast(I32),
+                in_=wg_scales[0, SCALE_ROWS * s:SCALE_ROWS * (s + 1), :].bitcast(I32),
             )
         nc.sync.dma_start(
             out=wg_codes[:].bitcast(I32),

from contextlib import ExitStack

import concourse.mybir as mybir
from concourse.masks import make_identity

K, N, T = 512, 512, 1536
FLOPS = 2 * 2 * K * N * T

F32 = mybir.dt.float32
BF16 = mybir.dt.bfloat16
I32 = mybir.dt.int32
U32 = mybir.dt.uint32
U8 = mybir.dt.uint8
FP8X4 = mybir.dt.float8_e4m3fn_x4
ACT = mybir.ActivationFunctionType
ALU = mybir.AluOpType

P = 128
PACK = 4
LINE = 4
WIDTH = 512
HALF = WIDTH // 2
GROUPS = N // P
CHUNKS = T // WIDTH
TILES = CHUNKS * GROUPS
LAST = TILES - 1
QUADRANT = 32
SCALE_ROWS = 4

assert CHUNKS == 3

SUM_BANKS = 2
H_BANKS = 4

TANH_LEAD = 2
CARRY_LEAD = 1
BLEND_LAG = 2

EARLY_RES = 3
LAST_CHUNK_STEP = 2
VECTOR_PRODUCTS = (1, 8)


def tile_mix_hway_tanh_none_kernel(tc, x, wg_words, wg_scales, wh, bg, res, out):
    nc = tc.nc
    with ExitStack() as ctx:
        sb = ctx.enter_context(tc.tile_pool(name="sb", bufs=1))
        ps = ctx.enter_context(tc.psum_pool(name="ps", bufs=1))
        ctx.enter_context(tc.manual_schedule())

        ident = sb.tile([P, P], F32, name="ident")
        make_identity(nc, ident[:])
        wg_scale_sb = sb.tile([P, N], U8, name="wg_scale_sb", align_bytes=64)
        nc.vector.memset(wg_scale_sb[:].bitcast(U32), 0)
        bias_rows = sb.tile([P, P], F32, name="bias_rows")
        nc.vector.memset(bias_rows[:], 0.0)

        def tokens(chunk):
            return slice(chunk * WIDTH, (chunk + 1) * WIDTH)

        def features(u):
            return slice(u % GROUPS * P, (u % GROUPS + 1) * P)

        raw = {}
        res_sb = {}

        def load_x(chunk):
            raw[chunk] = sb.tile([P, PACK, WIDTH], F32, name="x_raw%d" % chunk)
            nc.sync.dma_start(out=raw[chunk][:], in_=x.rearrange("(p i) t -> p i t", i=PACK)[:, :, tokens(chunk)])

        def load_res(u):
            res_sb[u] = sb.tile([P, WIDTH], F32, name="res%d" % u)
            nc.sync.dma_start(out=res_sb[u][:], in_=res[features(u), tokens(u // GROUPS)])

        wg_codes = sb.tile([P, N * PACK], U8, name="wg_codes", align_bytes=64)
        load_x(0)
        nc.sync.dma_start(out=bias_rows[0:GROUPS, :], in_=bg.rearrange("(g p) -> g p", p=P))
        for s in range(P // QUADRANT):
            nc.sync.dma_start(
                out=wg_scale_sb[QUADRANT * s:QUADRANT * s + SCALE_ROWS, :].bitcast(I32),
                in_=wg_scales[0, SCALE_ROWS * s:SCALE_ROWS * (s + 1), :].bitcast(I32),
            )
        nc.sync.dma_start(
            out=wg_codes[:].bitcast(I32),
            in_=wg_words[0].rearrange("p n i -> p (n i)").bitcast(I32),
        )
        raw["wh"] = sb.tile([P, PACK, N], F32, name="wh_raw")
        nc.sync.dma_start(out=raw["wh"][:], in_=wh.rearrange("(p i) n -> p i n", i=PACK))
        load_x(1)
        for u in range(EARLY_RES):
            load_res(u)
        load_x(CHUNKS - 1)
        for u in range(EARLY_RES, TILES):
            load_res(u)

        grouped = {}
        codes = {}
        scales = {}
        for key in list(range(CHUNKS)) + ["wh"]:
            codes[key] = sb.tile([P, WIDTH], U32, name="codes_%s" % key, align_bytes=64)
            scales[key] = sb.tile([P, WIDTH], U8, name="scales_%s" % key, align_bytes=64)

        def interleave(copy, key, half):
            grouped[key, half] = sb.tile(
                [P, HALF * PACK], BF16, name="grouped_%s_%d" % (key, half), align_bytes=64
            )
            copy(
                out=grouped[key, half][:].rearrange("p (c e i) -> p c i e", e=LINE, i=PACK),
                in_=raw[key][:, :, half * HALF:(half + 1) * HALF].rearrange("p i (c e) -> p c i e", e=LINE),
            )

        def quantize(key, half):
            cols = slice(half * HALF, (half + 1) * HALF)
            nc.vector.quantize_mx(
                out=codes[key][:, cols].bitcast(FP8X4), scales=scales[key][:, cols], in_=grouped[key, half][:]
            )

        def quantize_on_vector(key):
            for half in range(2):
                interleave(nc.vector.tensor_copy, key, half)
            for half in range(2):
                quantize(key, half)

        neg_bias = sb.tile([P, GROUPS], F32, name="neg_bias")
        ga = {}
        ha = {}
        carry = {}
        h_by_token = {}
        h_ps = {}
        diff = {}
        kept = {}
        out_sb = {}

        def gate_sum(u):
            ga[u] = ps.tile([P, WIDTH], F32, name="ga%d" % u, tag="ga%d" % (u % SUM_BANKS))
            group = u % GROUPS
            nc.tensor.matmul_mx(
                out=ga[u][:],
                lhsT=wg_codes[:, group * P * PACK:(group + 1) * P * PACK].bitcast(FP8X4),
                lhsT_scale=wg_scale_sb[:, features(u)],
                rhs=codes[u // GROUPS][:].bitcast(FP8X4),
                rhs_scale=scales[u // GROUPS][:],
                start=True,
                stop=True,
            )

        def value_sum(u):
            ha[u] = ps.tile([P, WIDTH], F32, name="ha%d" % u, tag="ha%d" % (u % SUM_BANKS))
            for b in range(WIDTH // P):
                block = slice(b * P, (b + 1) * P)
                nc.tensor.matmul_mx(
                    out=ha[u][:, block],
                    lhsT=codes[u // GROUPS][:, block].bitcast(FP8X4),
                    lhsT_scale=scales[u // GROUPS][:, block],
                    rhs=codes["wh"][:, features(u)].bitcast(FP8X4),
                    rhs_scale=scales["wh"][:, features(u)],
                    start=True,
                    stop=True,
                )

        def sigmoid(u):
            carry[u] = sb.tile([P, WIDTH], F32, name="carry%d" % u)
            group = u % GROUPS
            nc.scalar.activation(
                out=carry[u][:], in_=ga[u][:], func=ACT.Sigmoid, bias=neg_bias[:, group:group + 1], scale=-1.0
            )

        def tanh(u):
            h_by_token[u] = sb.tile([P, WIDTH], F32, name="h_by_token%d" % u)
            nc.scalar.activation(out=h_by_token[u][:], in_=ha[u][:], func=ACT.Tanh)

        def turn(u):
            h_ps[u] = ps.tile([P, WIDTH], F32, name="h_ps%d" % u, tag="h%d" % (u % H_BANKS))
            for b in range(WIDTH // P):
                block = slice(b * P, (b + 1) * P)
                nc.tensor.transpose(h_ps[u][:, block], h_by_token[u][:, block], ident[:])

        def subtract(u):
            diff[u] = sb.tile([P, WIDTH], F32, name="diff%d" % u)
            nc.vector.tensor_tensor(out=diff[u][:], in0=h_ps[u][:], in1=res_sb[u][:], op=ALU.subtract)

        def multiply(engine, u, lo=0, hi=WIDTH):
            if lo == 0:
                kept[u] = sb.tile([P, WIDTH], F32, name="kept%d" % u)
            engine.tensor_tensor(out=kept[u][:, lo:hi], in0=diff[u][:, lo:hi], in1=carry[u][:, lo:hi], op=ALU.mult)

        def blend(u, lo=0, hi=WIDTH):
            if lo == 0:
                out_sb[u] = sb.tile([P, WIDTH], F32, name="out%d" % u)
            nc.vector.tensor_tensor(
                out=out_sb[u][:, lo:hi], in0=h_ps[u][:, lo:hi], in1=kept[u][:, lo:hi], op=ALU.subtract
            )

        def store(u, lo=0, hi=WIDTH):
            nc.sync.dma_start(out=out[features(u), tokens(u // GROUPS)][:, lo:hi], in_=out_sb[u][:, lo:hi])

        quantize_on_vector(0)
        bias_ps = ps.tile([P, WIDTH], F32, name="bias_ps", tag="h%d" % (H_BANKS - 1))
        nc.tensor.transpose(bias_ps[:, 0:P], bias_rows[:], ident[:])
        nc.vector.tensor_scalar(out=neg_bias[:], in0=bias_ps[:, 0:GROUPS], scalar1=-1.0, scalar2=None, op0=ALU.mult)
        for u in range(GROUPS - 1):
            gate_sum(u)
            sigmoid(u)
        quantize_on_vector("wh")
        for u in range(TANH_LEAD):
            value_sum(u)
            tanh(u)
        quantize_on_vector(1)
        gate_sum(GROUPS - 1)
        sigmoid(GROUPS - 1)

        for u in range(TILES):
            turn(u)
            makes_tanh = u + TANH_LEAD < TILES
            makes_carry = GROUPS <= u + CARRY_LEAD < TILES
            if makes_tanh:
                value_sum(u + TANH_LEAD)
            if makes_carry:
                gate_sum(u + CARRY_LEAD)
            if makes_tanh:
                tanh(u + TANH_LEAD)
            if makes_carry:
                sigmoid(u + CARRY_LEAD)
            if 0 <= u - LAST_CHUNK_STEP < 2:
                interleave(nc.scalar.copy, CHUNKS - 1, u - LAST_CHUNK_STEP)
            subtract(u)
            if u not in VECTOR_PRODUCTS and u != LAST:
                multiply(nc.gpsimd, u)
            if u - 1 in VECTOR_PRODUCTS:
                multiply(nc.vector, u - 1)
            if 2 <= u - LAST_CHUNK_STEP < 4:
                quantize(CHUNKS - 1, u - LAST_CHUNK_STEP - 2)
            if u >= BLEND_LAG:
                blend(u - BLEND_LAG)

        multiply(nc.gpsimd, LAST, 0, HALF)
        for u in range(TILES - BLEND_LAG, LAST):
            blend(u)
        multiply(nc.vector, LAST, HALF, WIDTH)
        blend(LAST, 0, HALF)
        blend(LAST, HALF, WIDTH)

        for u in range(LAST):
            store(u)
        store(LAST, 0, HALF)
        store(LAST, HALF, WIDTH)
